import numpy as np
import ml_dtypes


def mxq(x, axis, fmt="e4m3"):
    dtype, down = {"e4m3": (ml_dtypes.float8_e4m3fn, 7), "e5m2": (ml_dtypes.float8_e5m2, 14)}[fmt]
    v = np.moveaxis(np.asarray(x, np.float32).astype(ml_dtypes.bfloat16).astype(np.float64), axis, -1)
    blocks = v.reshape(v.shape[:-1] + (-1, 32))
    amax = np.abs(blocks).max(-1, keepdims=True)
    byte = np.maximum(np.where(amax > 0, np.frexp(amax)[1] - 1 + 127, 0) - down, 1)
    scale = np.exp2(byte - 127.0)
    codes = (blocks / scale).astype(np.float32).astype(dtype).astype(np.float64)
    return np.moveaxis((codes * scale).reshape(v.shape), -1, axis)


WIDE = False


def mx_kscale(k):
    if not WIDE:
        return np.ones(k)
    levels = np.array([10, -10, 5, -5, 0])
    if k % 512:
        return np.exp2(np.random.permutation(np.resize(levels, k // 32))).repeat(32)
    a = np.empty((k // 512, 16))
    for p in range(k // 512):
        a[p, :8] = np.random.permutation(np.resize(levels, 8))
        for g in range(8):
            far = levels[np.abs(levels - a[p, g]) >= 10]
            a[p, g + 8] = far[np.random.randint(len(far))]
    return np.exp2(a.ravel()).repeat(32)


def f64(x):
    return np.asarray(x).astype(np.float64)


def striped8(idx):
    return np.asarray(idx).reshape(8, -1, 16).transpose(0, 2, 1).reshape(128, -1).astype(np.uint16)


def unstriped8(offs):
    return offs.reshape(8, 16, -1).transpose(0, 2, 1).reshape(8, -1).astype(np.int64)


def pick8(x, idx, run):
    r = np.arange(len(x))
    return x[r[:, None], idx[r % (8 * run) // run]]


E2M1 = np.array([0.0, 0.5, 1.0, 1.5, 2.0, 3.0, 4.0, 6.0, -0.0, -0.5, -1.0, -1.5, -2.0, -3.0, -4.0, -6.0])


def pack_weight(w, fmt):
    k, n = w.shape
    w = f64(np.asarray(w, np.float32).astype(ml_dtypes.bfloat16)).reshape(k // 32, 32, n)
    amax = np.abs(w).max(1)
    if fmt == "e4m3":
        byte = np.frexp(amax)[1] - 1 + 127 - 7
    else:
        mant, ex = np.frexp(amax / 6.0)
        byte = np.where(mant > 0.5, ex, ex - 1) + 127
    byte = np.clip(np.where(amax > 0, byte, 1), 1, 254)
    scaled = (w * np.exp2(127.0 - byte)[:, None, :]).reshape(k, n).astype(np.float32)
    by_word = np.ascontiguousarray(scaled.reshape(k // 512, 128, 4, n).transpose(0, 1, 3, 2))
    if fmt == "e4m3":
        words = by_word.astype(ml_dtypes.float8_e4m3fn).view(np.uint8)
    else:
        c = by_word.astype(ml_dtypes.float4_e2m1fn).view(np.uint8) & 0xF
        words = (c[..., 0::2] | (c[..., 1::2] << 4)).reshape(k // 512, 128, 2 * n)
    return np.ascontiguousarray(words), np.ascontiguousarray(byte.astype(np.uint8).reshape(k // 512, 16, n))


def unpack_weight(words, scales, fmt):
    g, _, n = scales.shape
    words = np.ascontiguousarray(words).reshape(g, 128, n, -1)
    if fmt == "e4m3":
        vals = words.view(ml_dtypes.float8_e4m3fn).astype(np.float64)
    else:
        nib = np.empty((g, 128, n, 4), np.uint8)
        nib[..., 0::2] = words & 0xF
        nib[..., 1::2] = words >> 4
        vals = E2M1[nib]
    vals = vals * np.repeat(np.exp2(scales.astype(np.float64) - 127.0), 8, axis=1)[..., None]
    return vals.transpose(0, 1, 3, 2).reshape(g * 512, n)


D, T, I, Q, G = 512, 1024, 512, 128, 64


def setup_inputs():
    n = np.random.standard_normal
    idx = np.stack([np.random.permutation(T)[:I] for _ in range(8)])
    idx2 = np.stack([np.random.permutation(T)[:I] for _ in range(8)])
    idx4 = np.stack([np.random.permutation(T)[:I] for _ in range(8)])
    fd = mx_kscale(D)
    keysp = pack_weight(n((D, T)) / fd[:, None], "e4m3")
    return {
        "query": (n((D, Q)) * 0.9 / np.sqrt(D) * fd[:, None]).astype(np.float32),
        "query2": (n((D, Q)) * 0.9 / np.sqrt(D) * fd[:, None]).astype(np.float32),
        "keys_words": keysp[0],
        "keys_scales": keysp[1],
        "lam": (np.random.uniform(0.5, 1.5, (Q, 1))).astype(np.float32),
        "bar": (np.random.uniform(0.6, 1.0, (Q, 1))).astype(np.float32),
        "reserve": (np.random.uniform(20.0, 80.0, (Q, 1))).astype(np.float32),
        "old": (np.random.uniform(0.0, 2.0, (Q, T))).astype(np.float32),
        "gainm": (np.random.uniform(0.5, 1.5, (Q, I))).astype(np.float32),
        "offs": striped8(idx),
        "offs2": striped8(idx2),
        "offs4": striped8(idx4),
    }


def reference(query, query2, keys_words, keys_scales, lam, bar, reserve, old, gainm, offs, offs2, offs4):
    idx = unstriped8(offs)
    idx2 = unstriped8(offs2)
    idx4 = unstriped8(offs4)
    keysu = unpack_weight(keys_words, keys_scales, "e4m3")
    queryq = mxq(f64(query), 0, "e4m3")
    a = queryq.T @ keysu
    query2q = mxq(f64(query2), 0, "e4m3")
    b = query2q.T @ keysu
    s = pick8(a, idx, 16) + pick8(a, idx2, 16) * np.tanh(pick8(b, idx, 16)) * f64(lam)
    p = np.exp(s)
    pm = p.reshape(Q, G, I // G).mean(axis=2)
    pr = np.repeat(pm, I // G, axis=1)
    r = np.maximum(p - pr * f64(bar), 0.0)
    w = r / (np.sum(r, axis=1, keepdims=True) + f64(reserve))
    ws = w * f64(gainm) * 256.0
    wf = np.zeros((Q, T))
    wf[np.arange(Q)[:, None], idx4[np.arange(Q) % 128 // 16]] = ws
    y = f64(old) + wf
    return y

@@ -1,0 +1,175 @@
+from contextlib import ExitStack
+
+import concourse.mybir as mybir
+
+D, T, I, Q, RUN = 512, 1024, 512, 128, 8
+FLOPS = 2 * 2 * D * Q * T
+
+F32 = mybir.dt.float32
+BF16 = mybir.dt.bfloat16
+I32 = mybir.dt.int32
+U32 = mybir.dt.uint32
+U16 = mybir.dt.uint16
+U8 = mybir.dt.uint8
+FP8X4 = mybir.dt.float8_e4m3fn_x4
+ALU = mybir.AluOpType
+ACT = mybir.ActivationFunctionType
+
+P = 128
+PACK = 4
+BANK = 512
+HALF = I // 2
+PIECE = 256
+OUT_WIDTHS = (128, 384, 384, 128)
+
+
+def tile_attend_turnedby_abovepage_moved_heads_kernel(
+    tc, query, query2, keys_words, keys_scales, lam, bar, reserve, old, gainm, offs, offs2, offs4, out
+):
+    nc = tc.nc
+    with ExitStack() as ctx:
+        sb = ctx.enter_context(tc.tile_pool(name="sb", bufs=1))
+        psum = ctx.enter_context(tc.psum_pool(name="psum", bufs=1))
+
+        key_scales = sb.tile([P, PIECE], U8, name="key_scales", align_bytes=64)
+        for quad in range(4):
+            queue = nc.scalar
+            queue.dma_start(
+                out=key_scales[32 * quad : 32 * quad + 16, :].bitcast(I32),
+                in_=keys_scales[0][4 * quad : 4 * quad + 4, :].bitcast(I32).rearrange("r (j c) -> j r c", j=4),
+            )
+
+        words = keys_words[0].rearrange("p n t -> p (n t)")
+        raw_b = sb.tile([P, PACK, Q], F32, name="raw_b", tag="slot_b")
+        raw_a = sb.tile([P, PACK, Q], F32, name="raw_a", tag="slot_a")
+        key_words = [sb.tile([P, BANK], U32, name=f"key_words{h}", align_bytes=64) for h in range(2)]
+        nc.sync.dma_start(out=raw_b[:], in_=query2.rearrange("(p j) q -> p j q", j=PACK))
+        nc.sync.dma_start(out=key_words[0][:].bitcast(I32), in_=words[:, 0 : PACK * BANK].bitcast(I32))
+        nc.sync.dma_start(out=raw_a[:], in_=query.rearrange("(p j) q -> p j q", j=PACK))
+        nc.sync.dma_start(out=key_words[1][:].bitcast(I32), in_=words[:, PACK * BANK : 2 * PACK * BANK].bitcast(I32))
+
+        list1 = sb.tile([P, I // 16], U16, name="list1")
+        list2 = sb.tile([P, I // 16], U16, name="list2")
+        list4 = sb.tile([P, I // 16], U16, name="list4")
+        nc.sync.dma_start(list1[:], offs)
+        nc.sync.dma_start(list2[:], offs2)
+        nc.sync.dma_start(list4[:], offs4)
+
+        lam_col = sb.tile([P, 1], F32, name="lam_col")
+        bar_col = sb.tile([P, 1], F32, name="bar_col")
+        reserve_col = sb.tile([P, 1], F32, name="reserve_col")
+        nc.gpsimd.dma_start(out=lam_col[:], in_=lam)
+        nc.gpsimd.dma_start(out=bar_col[:], in_=bar)
+        nc.gpsimd.dma_start(out=reserve_col[:], in_=reserve)
+        cut = sb.tile([P, 1], F32, name="cut")
+        nc.gpsimd.tensor_scalar(cut[:], bar_col[:], -1.0 / RUN, 0.0, ALU.mult, ALU.add)
+
+        placed = sb.tile([P, T], F32, name="placed")
+        nc.vector.memset(placed[:], 0.0)
+
+        grouped_b = sb.tile([P, Q, PACK], BF16, name="grouped_b", align_bytes=64)
+        grouped_a = sb.tile([P, Q, PACK], BF16, name="grouped_a", align_bytes=64)
+        codes_b = sb.tile([P, Q], U32, name="codes_b", align_bytes=64)
+        codes_a = sb.tile([P, Q], U32, name="codes_a", align_bytes=64)
+        scales_b = sb.tile([P, Q], U8, name="scales_b", align_bytes=64)
+        scales_a = sb.tile([P, Q], U8, name="scales_a", align_bytes=64)
+
+        nc.vector.tensor_copy(
+            out=grouped_b[:].rearrange("p (c i) t -> p c t i", i=4),
+            in_=raw_b[:].rearrange("p t (c i) -> p c t i", i=4),
+        )
+        nc.vector.quantize_mx(
+            out=codes_b[:].bitcast(FP8X4), scales=scales_b[:], in_=grouped_b[:].rearrange("p q t -> p (q t)")
+        )
+        nc.vector.tensor_copy(
+            out=grouped_a[:].rearrange("p (c i) t -> p c t i", i=4),
+            in_=raw_a[:].rearrange("p t (c i) -> p c t i", i=4),
+        )
+        nc.vector.quantize_mx(
+            out=codes_a[:].bitcast(FP8X4), scales=scales_a[:], in_=grouped_a[:].rearrange("p q t -> p (q t)")
+        )
+
+        gain = sb.tile([P, I], F32, name="gain", tag="slot_b")
+        nc.sync.dma_start(out=gain[:], in_=gainm)
+        counts = sb.tile([P, T], F32, name="counts", tag="slot_a")
+        nc.sync.dma_start(out=counts[:], in_=old)
+
+        a_all = sb.tile([P, T], F32, name="a_all")
+        b_all = sb.tile([P, T], F32, name="b_all")
+
+        def score(codes, scales, piece, dest):
+            h, c0 = divmod(piece * PIECE, BANK)
+            nc.tensor.matmul_mx(
+                out=dest,
+                lhsT=codes[:].bitcast(FP8X4),
+                lhsT_scale=scales[:],
+                rhs=key_words[h][:, c0 : c0 + PIECE].bitcast(FP8X4),
+                rhs_scale=key_scales[4 * piece : P, :],
+                start=True,
+                stop=True,
+            )
+
+        for piece in range(4):
+            bank = psum.tile([P, PIECE], F32, name=f"bank_b{piece}")
+            score(codes_b, scales_b, piece, bank[:])
+            columns = b_all[:, piece * PIECE : (piece + 1) * PIECE]
+            if piece < 3:
+                nc.scalar.activation(columns, bank[:], ACT.Copy)
+            else:
+                nc.vector.tensor_copy(out=columns, in_=bank[:])
+        for h in range(2):
+            bank = psum.tile([P, BANK], F32, name=f"bank_a{h}")
+            for u in range(2):
+                score(codes_a, scales_a, 2 * h + u, bank[:, u * PIECE : (u + 1) * PIECE])
+            nc.vector.tensor_copy(out=a_all[:, h * BANK : (h + 1) * BANK], in_=bank[:])
+
+        def half_tiles(name, width=HALF):
+            return [sb.tile([P, width], F32, name=f"{name}{h}") for h in range(2)]
+
+        b_picked, turn, a_first, turned = half_tiles("b_picked"), half_tiles("turn"), half_tiles("a_first"), half_tiles("turned")
+        score_s, p = half_tiles("score_s"), half_tiles("p")
+        above = sb.tile([P, I], F32, name="above")
+        run_sum = half_tiles("run_sum", HALF // RUN)
+        part = sb.tile([P, I], F32, name="part")
+        cols = [slice(h * HALF // 16, (h + 1) * HALF // 16) for h in range(2)]
+
+        for h in range(2):
+            nc.scalar.activation(b_picked[h][:], b_all[:].indirect(list1[:, cols[h]]), ACT.Copy)
+            nc.scalar.activation(turn[h][:], b_picked[h][:], ACT.Tanh)
+        for h in range(2):
+            nc.vector.tensor_tensor(turned[h][:], a_all[:].indirect(list2[:, cols[h]]), turn[h][:], ALU.mult)
+        for h in range(2):
+            nc.scalar.activation(a_first[h][:], a_all[:].indirect(list1[:, cols[h]]), ACT.Copy)
+        for h in range(2):
+            nc.vector.scalar_tensor_tensor(score_s[h][:], turned[h][:], lam_col[:], a_first[h][:], ALU.mult, ALU.add)
+        for h in range(2):
+            nc.scalar.activation(p[h][:], score_s[h][:], ACT.Exp)
+        runs = [p[h][:].rearrange("p (g j) -> p g j", j=RUN) for h in range(2)]
+        for h in range(2):
+            nc.vector.tensor_reduce(run_sum[h][:], runs[h], mybir.AxisListType.X, ALU.add)
+        for h in range(2):
+            nc.vector.scalar_tensor_tensor(
+                above[:, h * HALF : (h + 1) * HALF].rearrange("p (g j) -> p g j", j=RUN),
+                run_sum[h][:].unsqueeze(2).to_broadcast([P, HALF // RUN, RUN]),
+                cut[:],
+                runs[h],
+                ALU.mult,
+                ALU.add,
+            )
+        total = sb.tile([P, 1], F32, name="total")
+        inverse = sb.tile([P, 1], F32, name="inverse")
+        nc.vector.tensor_scalar(part[:], above[:], 0.0, reserve_col[:], ALU.max, ALU.add, accum_out=total[:])
+        nc.vector.reciprocal(inverse[:], total[:])
+        factor = sb.tile([P, I], F32, name="factor")
+        nc.vector.tensor_scalar(factor[:], gain[:], inverse[:], 256.0, ALU.mult, ALU.mult)
+        nc.vector.tensor_tensor(placed[:].indirect(list4[:]), part[:], factor[:], ALU.mult)
+
+        first = 0
+        for n, width in enumerate(OUT_WIDTHS):
+            result = sb.tile([P, width], F32, name=f"result{n}")
+            nc.vector.tensor_tensor(
+                result[:], placed[:, first : first + width], counts[:, first : first + width], ALU.add
+            )
+            queue = nc.sync if n % 2 == 0 else nc.scalar
+            queue.dma_start(out=out[:, first : first + width], in_=result[:])
+            first += width

@@ -32,18 +32,22 @@ def tile_attend_turnedby_abovepage_moved_heads_kernel(
         psum = ctx.enter_context(tc.psum_pool(name="psum", bufs=1))
 
         key_scales = sb.tile([P, PIECE], U8, name="key_scales", align_bytes=64)
-        for quad in range(4):
-            queue = nc.scalar
+
+        def load_scales(queue, quad):
             queue.dma_start(
                 out=key_scales[32 * quad : 32 * quad + 16, :].bitcast(I32),
                 in_=keys_scales[0][4 * quad : 4 * quad + 4, :].bitcast(I32).rearrange("r (j c) -> j r c", j=4),
             )
+
+        for quad in range(3):
+            load_scales(nc.scalar, quad)
 
         words = keys_words[0].rearrange("p n t -> p (n t)")
         raw_b = sb.tile([P, PACK, Q], F32, name="raw_b", tag="slot_b")
         raw_a = sb.tile([P, PACK, Q], F32, name="raw_a", tag="slot_a")
         key_words = [sb.tile([P, BANK], U32, name=f"key_words{h}", align_bytes=64) for h in range(2)]
         nc.sync.dma_start(out=raw_b[:], in_=query2.rearrange("(p j) q -> p j q", j=PACK))
+        load_scales(nc.sync, 3)
         nc.sync.dma_start(out=key_words[0][:].bitcast(I32), in_=words[:, 0 : PACK * BANK].bitcast(I32))
         nc.sync.dma_start(out=raw_a[:], in_=query.rearrange("(p j) q -> p j q", j=PACK))
         nc.sync.dma_start(out=key_words[1][:].bitcast(I32), in_=words[:, PACK * BANK : 2 * PACK * BANK].bitcast(I32))
@@ -58,11 +62,11 @@ def tile_attend_turnedby_abovepage_moved_heads_kernel(
         lam_col = sb.tile([P, 1], F32, name="lam_col")
         bar_col = sb.tile([P, 1], F32, name="bar_col")
         reserve_col = sb.tile([P, 1], F32, name="reserve_col")
-        nc.gpsimd.dma_start(out=lam_col[:], in_=lam)
         nc.gpsimd.dma_start(out=bar_col[:], in_=bar)
+        nc.gpsimd.dma_start(out=lam_col[:], in_=lam)
         nc.gpsimd.dma_start(out=reserve_col[:], in_=reserve)
         cut = sb.tile([P, 1], F32, name="cut")
-        nc.gpsimd.tensor_scalar(cut[:], bar_col[:], -1.0 / RUN, 0.0, ALU.mult, ALU.add)
+        nc.scalar.activation(cut[:], bar_col[:], ACT.Copy, scale=-1.0 / RUN)
 
         placed = sb.tile([P, T], F32, name="placed")
         nc.vector.memset(placed[:], 0.0)
@@ -126,7 +130,8 @@ def tile_attend_turnedby_abovepage_moved_heads_kernel(
         def half_tiles(name, width=HALF):
             return [sb.tile([P, width], F32, name=f"{name}{h}") for h in range(2)]
 
-        b_picked, turn, a_first, turned = half_tiles("b_picked"), half_tiles("turn"), half_tiles("a_first"), half_tiles("turned")
+        b_picked = [sb.tile([P, HALF], F32, name=f"b_picked{h}", tag=f"picked{h}") for h in range(2)]
+        turn, turned = half_tiles("turn"), half_tiles("turned")
         score_s, p = half_tiles("score_s"), half_tiles("p")
         above = sb.tile([P, I], F32, name="above")
         run_sum = half_tiles("run_sum", HALF // RUN)
@@ -138,6 +143,7 @@ def tile_attend_turnedby_abovepage_moved_heads_kernel(
             nc.scalar.activation(turn[h][:], b_picked[h][:], ACT.Tanh)
         for h in range(2):
             nc.vector.tensor_tensor(turned[h][:], a_all[:].indirect(list2[:, cols[h]]), turn[h][:], ALU.mult)
+        a_first = [sb.tile([P, HALF], F32, name=f"a_first{h}", tag=f"picked{h}") for h in range(2)]
         for h in range(2):
             nc.scalar.activation(a_first[h][:], a_all[:].indirect(list1[:, cols[h]]), ACT.Copy)
         for h in range(2):

@@ -20,7 +20,7 @@ PACK = 4
 BANK = 512
 HALF = I // 2
 PIECE = 256
-OUT_WIDTHS = (128, 384, 384, 128)
+OUT_WIDTHS = (128, 256, 256, 256, 128)
 
 
 def tile_attend_turnedby_abovepage_moved_heads_kernel(
@@ -62,9 +62,9 @@ def tile_attend_turnedby_abovepage_moved_heads_kernel(
         lam_col = sb.tile([P, 1], F32, name="lam_col")
         bar_col = sb.tile([P, 1], F32, name="bar_col")
         reserve_col = sb.tile([P, 1], F32, name="reserve_col")
-        nc.gpsimd.dma_start(out=bar_col[:], in_=bar)
-        nc.gpsimd.dma_start(out=lam_col[:], in_=lam)
-        nc.gpsimd.dma_start(out=reserve_col[:], in_=reserve)
+        nc.sync.dma_start(out=bar_col[:], in_=bar)
+        nc.sync.dma_start(out=lam_col[:], in_=lam)
+        nc.sync.dma_start(out=reserve_col[:], in_=reserve)
         cut = sb.tile([P, 1], F32, name="cut")
         nc.scalar.activation(cut[:], bar_col[:], ACT.Copy, scale=-1.0 / RUN)
 

from contextlib import ExitStack

import concourse.mybir as mybir

D, T, I, Q, RUN = 512, 1024, 512, 128, 8
FLOPS = 2 * 2 * D * Q * T

F32 = mybir.dt.float32
BF16 = mybir.dt.bfloat16
I32 = mybir.dt.int32
U32 = mybir.dt.uint32
U16 = mybir.dt.uint16
U8 = mybir.dt.uint8
FP8X4 = mybir.dt.float8_e4m3fn_x4
ALU = mybir.AluOpType
ACT = mybir.ActivationFunctionType

P = 128
PACK = 4
BANK = 512
HALF = I // 2
PIECE = 256
OUT_WIDTHS = (128, 256, 256, 256, 128)


def tile_attend_turnedby_abovepage_moved_heads_kernel(
    tc, query, query2, keys_words, keys_scales, lam, bar, reserve, old, gainm, offs, offs2, offs4, out
):
    nc = tc.nc
    with ExitStack() as ctx:
        sb = ctx.enter_context(tc.tile_pool(name="sb", bufs=1))
        psum = ctx.enter_context(tc.psum_pool(name="psum", bufs=1))

        key_scales = sb.tile([P, PIECE], U8, name="key_scales", align_bytes=64)

        def load_scales(queue, quad):
            queue.dma_start(
                out=key_scales[32 * quad : 32 * quad + 16, :].bitcast(I32),
                in_=keys_scales[0][4 * quad : 4 * quad + 4, :].bitcast(I32).rearrange("r (j c) -> j r c", j=4),
            )

        for quad in range(3):
            load_scales(nc.scalar, quad)

        words = keys_words[0].rearrange("p n t -> p (n t)")
        raw_b = sb.tile([P, PACK, Q], F32, name="raw_b", tag="slot_b")
        raw_a = sb.tile([P, PACK, Q], F32, name="raw_a", tag="slot_a")
        key_words = [sb.tile([P, BANK], U32, name=f"key_words{h}", align_bytes=64) for h in range(2)]
        nc.sync.dma_start(out=raw_b[:], in_=query2.rearrange("(p j) q -> p j q", j=PACK))
        load_scales(nc.sync, 3)
        nc.sync.dma_start(out=key_words[0][:].bitcast(I32), in_=words[:, 0 : PACK * BANK].bitcast(I32))
        nc.sync.dma_start(out=raw_a[:], in_=query.rearrange("(p j) q -> p j q", j=PACK))
        nc.sync.dma_start(out=key_words[1][:].bitcast(I32), in_=words[:, PACK * BANK : 2 * PACK * BANK].bitcast(I32))

        list1 = sb.tile([P, I // 16], U16, name="list1")
        list2 = sb.tile([P, I // 16], U16, name="list2")
        list4 = sb.tile([P, I // 16], U16, name="list4")
        nc.sync.dma_start(list1[:], offs)
        nc.sync.dma_start(list2[:], offs2)
        nc.sync.dma_start(list4[:], offs4)

        lam_col = sb.tile([P, 1], F32, name="lam_col")
        bar_col = sb.tile([P, 1], F32, name="bar_col")
        reserve_col = sb.tile([P, 1], F32, name="reserve_col")
        nc.sync.dma_start(out=bar_col[:], in_=bar)
        nc.sync.dma_start(out=lam_col[:], in_=lam)
        nc.sync.dma_start(out=reserve_col[:], in_=reserve)
        cut = sb.tile([P, 1], F32, name="cut")
        nc.scalar.activation(cut[:], bar_col[:], ACT.Copy, scale=-1.0 / RUN)

        placed = sb.tile([P, T], F32, name="placed")
        nc.vector.memset(placed[:], 0.0)

        grouped_b = sb.tile([P, Q, PACK], BF16, name="grouped_b", align_bytes=64)
        grouped_a = sb.tile([P, Q, PACK], BF16, name="grouped_a", align_bytes=64)
        codes_b = sb.tile([P, Q], U32, name="codes_b", align_bytes=64)
        codes_a = sb.tile([P, Q], U32, name="codes_a", align_bytes=64)
        scales_b = sb.tile([P, Q], U8, name="scales_b", align_bytes=64)
        scales_a = sb.tile([P, Q], U8, name="scales_a", align_bytes=64)

        nc.vector.tensor_copy(
            out=grouped_b[:].rearrange("p (c i) t -> p c t i", i=4),
            in_=raw_b[:].rearrange("p t (c i) -> p c t i", i=4),
        )
        nc.vector.quantize_mx(
            out=codes_b[:].bitcast(FP8X4), scales=scales_b[:], in_=grouped_b[:].rearrange("p q t -> p (q t)")
        )
        nc.vector.tensor_copy(
            out=grouped_a[:].rearrange("p (c i) t -> p c t i", i=4),
            in_=raw_a[:].rearrange("p t (c i) -> p c t i", i=4),
        )
        nc.vector.quantize_mx(
            out=codes_a[:].bitcast(FP8X4), scales=scales_a[:], in_=grouped_a[:].rearrange("p q t -> p (q t)")
        )

        gain = sb.tile([P, I], F32, name="gain", tag="slot_b")
        nc.sync.dma_start(out=gain[:], in_=gainm)
        counts = sb.tile([P, T], F32, name="counts", tag="slot_a")
        nc.sync.dma_start(out=counts[:], in_=old)

        a_all = sb.tile([P, T], F32, name="a_all")
        b_all = sb.tile([P, T], F32, name="b_all")

        def score(codes, scales, piece, dest):
            h, c0 = divmod(piece * PIECE, BANK)
            nc.tensor.matmul_mx(
                out=dest,
                lhsT=codes[:].bitcast(FP8X4),
                lhsT_scale=scales[:],
                rhs=key_words[h][:, c0 : c0 + PIECE].bitcast(FP8X4),
                rhs_scale=key_scales[4 * piece : P, :],
                start=True,
                stop=True,
            )

        for piece in range(4):
            bank = psum.tile([P, PIECE], F32, name=f"bank_b{piece}")
            score(codes_b, scales_b, piece, bank[:])
            columns = b_all[:, piece * PIECE : (piece + 1) * PIECE]
            if piece < 3:
                nc.scalar.activation(columns, bank[:], ACT.Copy)
            else:
                nc.vector.tensor_copy(out=columns, in_=bank[:])
        for h in range(2):
            bank = psum.tile([P, BANK], F32, name=f"bank_a{h}")
            for u in range(2):
                score(codes_a, scales_a, 2 * h + u, bank[:, u * PIECE : (u + 1) * PIECE])
            nc.vector.tensor_copy(out=a_all[:, h * BANK : (h + 1) * BANK], in_=bank[:])

        def half_tiles(name, width=HALF):
            return [sb.tile([P, width], F32, name=f"{name}{h}") for h in range(2)]

        b_picked = [sb.tile([P, HALF], F32, name=f"b_picked{h}", tag=f"picked{h}") for h in range(2)]
        turn, turned = half_tiles("turn"), half_tiles("turned")
        score_s, p = half_tiles("score_s"), half_tiles("p")
        above = sb.tile([P, I], F32, name="above")
        run_sum = half_tiles("run_sum", HALF // RUN)
        part = sb.tile([P, I], F32, name="part")
        cols = [slice(h * HALF // 16, (h + 1) * HALF // 16) for h in range(2)]

        for h in range(2):
            nc.scalar.activation(b_picked[h][:], b_all[:].indirect(list1[:, cols[h]]), ACT.Copy)
            nc.scalar.activation(turn[h][:], b_picked[h][:], ACT.Tanh)
        for h in range(2):
            nc.vector.tensor_tensor(turned[h][:], a_all[:].indirect(list2[:, cols[h]]), turn[h][:], ALU.mult)
        a_first = [sb.tile([P, HALF], F32, name=f"a_first{h}", tag=f"picked{h}") for h in range(2)]
        for h in range(2):
            nc.scalar.activation(a_first[h][:], a_all[:].indirect(list1[:, cols[h]]), ACT.Copy)
        for h in range(2):
            nc.vector.scalar_tensor_tensor(score_s[h][:], turned[h][:], lam_col[:], a_first[h][:], ALU.mult, ALU.add)
        for h in range(2):
            nc.scalar.activation(p[h][:], score_s[h][:], ACT.Exp)
        runs = [p[h][:].rearrange("p (g j) -> p g j", j=RUN) for h in range(2)]
        for h in range(2):
            nc.vector.tensor_reduce(run_sum[h][:], runs[h], mybir.AxisListType.X, ALU.add)
        for h in range(2):
            nc.vector.scalar_tensor_tensor(
                above[:, h * HALF : (h + 1) * HALF].rearrange("p (g j) -> p g j", j=RUN),
                run_sum[h][:].unsqueeze(2).to_broadcast([P, HALF // RUN, RUN]),
                cut[:],
                runs[h],
                ALU.mult,
                ALU.add,
            )
        total = sb.tile([P, 1], F32, name="total")
        inverse = sb.tile([P, 1], F32, name="inverse")
        nc.vector.tensor_scalar(part[:], above[:], 0.0, reserve_col[:], ALU.max, ALU.add, accum_out=total[:])
        nc.vector.reciprocal(inverse[:], total[:])
        factor = sb.tile([P, I], F32, name="factor")
        nc.vector.tensor_scalar(factor[:], gain[:], inverse[:], 256.0, ALU.mult, ALU.mult)
        nc.vector.tensor_tensor(placed[:].indirect(list4[:]), part[:], factor[:], ALU.mult)

        first = 0
        for n, width in enumerate(OUT_WIDTHS):
            result = sb.tile([P, width], F32, name=f"result{n}")
            nc.vector.tensor_tensor(
                result[:], placed[:, first : first + width], counts[:, first : first + width], ALU.add
            )
            queue = nc.sync if n % 2 == 0 else nc.scalar
            queue.dma_start(out=out[:, first : first + width], in_=result[:])
            first += width
